import numpy as np
import ml_dtypes


def mxq(x, axis, fmt="e4m3"):
    dtype, down = {"e4m3": (ml_dtypes.float8_e4m3fn, 7), "e5m2": (ml_dtypes.float8_e5m2, 14)}[fmt]
    v = np.moveaxis(np.asarray(x, np.float32).astype(ml_dtypes.bfloat16).astype(np.float64), axis, -1)
    blocks = v.reshape(v.shape[:-1] + (-1, 32))
    amax = np.abs(blocks).max(-1, keepdims=True)
    byte = np.maximum(np.where(amax > 0, np.frexp(amax)[1] - 1 + 127, 0) - down, 1)
    scale = np.exp2(byte - 127.0)
    codes = (blocks / scale).astype(np.float32).astype(dtype).astype(np.float64)
    return np.moveaxis((codes * scale).reshape(v.shape), -1, axis)


WIDE = False


def mx_kscale(k):
    if not WIDE:
        return np.ones(k)
    levels = np.array([10, -10, 5, -5, 0])
    if k % 512:
        return np.exp2(np.random.permutation(np.resize(levels, k // 32))).repeat(32)
    a = np.empty((k // 512, 16))
    for p in range(k // 512):
        a[p, :8] = np.random.permutation(np.resize(levels, 8))
        for g in range(8):
            far = levels[np.abs(levels - a[p, g]) >= 10]
            a[p, g + 8] = far[np.random.randint(len(far))]
    return np.exp2(a.ravel()).repeat(32)


def f64(x):
    return np.asarray(x).astype(np.float64)


def striped(idx):
    return np.tile(idx.reshape(-1, 16).T, (8, 1)).astype(np.uint16)


def unstriped(offs):
    return offs[:16].T.reshape(-1).astype(np.int64)


def striped8(idx):
    return np.concatenate([x.reshape(-1, 16).T for x in idx]).astype(np.uint16)


def runs(offs, k):
    lists = np.stack([offs[16 * r : 16 * r + 16].T.reshape(-1) for r in range(8)]).astype(np.int64)
    return lists[np.arange(k) % 512 // 64]


def pack_weight(w):
    k, n = w.shape
    w = f64(np.asarray(w, np.float32).astype(ml_dtypes.bfloat16)).reshape(k // 32, 32, n)
    amax = np.abs(w).max(1)
    byte = np.clip(np.where(amax > 0, np.frexp(amax)[1] - 1 + 127 - 7, 1), 1, 254)
    scaled = (w * np.exp2(127.0 - byte)[:, None, :]).reshape(k, n).astype(np.float32)
    words = np.ascontiguousarray(scaled.reshape(k // 512, 128, 4, n).transpose(0, 1, 3, 2)).astype(ml_dtypes.float8_e4m3fn).view(np.uint8)
    return words, np.ascontiguousarray(byte.astype(np.uint8).reshape(k // 512, 16, n))


def unpack_weight(words, scales):
    g, p, n, _ = words.shape
    vals = np.ascontiguousarray(words).view(ml_dtypes.float8_e4m3fn).astype(np.float64) * np.repeat(np.exp2(scales.astype(np.float64) - 127.0), 8, axis=1)[..., None]
    return vals.transpose(0, 1, 3, 2).reshape(g * 512, n)


def sigmoid(v):
    return 1.0 / (1.0 + np.exp(-np.maximum(v, -700.0)))


K, T, S, V, H = 512, 2048, 512, 512, 512


def setup_inputs():
    n = np.random.standard_normal
    s = mx_kscale(K)[:, None]
    u = mx_kscale(S)
    packed_xT = pack_weight(n((K, T)) * s)
    return {
        "x_words": packed_xT[0],
        "x_scales": packed_xT[1],
        "w1": (n((K, H)) / np.sqrt(K) / s).astype(np.float32),
        "w2": (n((K, H)) / np.sqrt(K) / s).astype(np.float32),
        "ga": (np.random.uniform(0.5, 1.5, (H, 1)) * u[:, None]).astype(np.float32),
        "gb": (np.random.uniform(0.5, 1.5, (H, 1)) / u[:, None]).astype(np.float32),
        "offs": striped(np.random.permutation(T)[:S]),
        "two": striped(np.random.permutation(T)[:V]),
        "n1": striped8(np.stack([np.random.permutation(S) for _ in range(8)])),
        "n2": striped8(np.stack([np.random.permutation(S) for _ in range(8)])),
        "nq": striped8(np.stack([np.random.permutation(V) for _ in range(8)])),
        "cq": striped8(np.stack([np.random.permutation(V) for _ in range(8)])),
    }


def reference(x_words, x_scales, w1, w2, ga, gb, offs, two, n1, n2, nq, cq):
    xq = unpack_weight(x_words, x_scales)[:, unstriped(offs)]
    a = mxq(f64(w1), 0, "e4m3").T @ xq
    k1 = a[np.arange(H)[:, None], runs(n1, H)]
    k2 = a[np.arange(H)[:, None], runs(n2, H)]
    z = f64(ga) * (np.maximum(np.minimum(a, k1), np.minimum(np.maximum(a, k1), k2)))
    x_two = unpack_weight(x_words, x_scales)[:, unstriped(two)]
    b = mxq(f64(w2), 0, "e4m3").T @ x_two
    z2 = f64(gb) * (b * (sigmoid(b[np.arange(H)[:, None], runs(nq, H)])))
    s = 0.0625 * ((mxq(z, 0, "e4m3").T @ mxq(z2, 0, "e4m3")))
    return s - (0.5 * (s[np.arange(S)[:, None], runs(cq, S)]))

@@ -1,0 +1,157 @@
+from contextlib import ExitStack
+
+import concourse.mybir as mybir
+
+K, T, S, V, H = 512, 2048, 512, 512, 512
+FLOPS = 2 * K * H * S + 2 * K * H * V + 2 * H * S * V
+
+F32 = mybir.dt.float32
+BF16 = mybir.dt.bfloat16
+I32 = mybir.dt.int32
+U32 = mybir.dt.uint32
+U16 = mybir.dt.uint16
+U8 = mybir.dt.uint8
+FP8X4 = mybir.dt.float8_e4m3fn_x4
+ALU = mybir.AluOpType
+ACT = mybir.ActivationFunctionType
+
+P = 128
+PACK = 4
+WINDOW = 1024
+
+
+def tile_picked_keymed_none_p_kernel(tc, x_words, x_scales, w1, w2, ga, gb, offs, two, n1, n2, nq, cq, out):
+    nc = tc.nc
+    with ExitStack() as ctx:
+        keep = ctx.enter_context(tc.tile_pool(name="keep", bufs=1))
+        psum = ctx.enter_context(tc.psum_pool(name="psum", bufs=1))
+
+        def sb(name, shape, dtype, tag=None):
+            return keep.tile(shape, dtype, name=name, tag=tag or name, align_bytes=64)
+
+        def load_list(name, src):
+            t = keep.tile([P, 32], U16, name=name)
+            nc.sync.dma_start(t[:], src)
+            return t
+
+        scale_table = sb("scale_table", [P, T], U8)
+        nc.vector.memset(scale_table[:].bitcast(I32), 0)
+        warm = sb("warm", [P, 2], F32)
+        nc.gpsimd.memset(warm[:, 0:1], 0.0)
+        nc.scalar.activation(warm[:, 1:2], warm[:, 0:1], ACT.Sigmoid)
+
+        offs_t = load_list("offs_t", offs)
+        two_t = load_list("two_t", two)
+        for q in range(4):
+            nc.sync.dma_start(scale_table[32 * q : 32 * q + 4, :].bitcast(I32), x_scales[0, 4 * q : 4 * q + 4, :].bitcast(I32))
+        w1_raw = sb("w1_raw", [P, PACK, H], F32)
+        nc.sync.dma_start(w1_raw[:], w1.rearrange("(p j) c -> p j c", j=PACK))
+        word_table = sb("word_table", [P, T], U32)
+        nc.sync.dma_start(word_table[:].bitcast(I32), x_words[0].rearrange("p c r -> p (c r)").bitcast(I32))
+        n1_t = load_list("n1_t", n1)
+        n2_t = load_list("n2_t", n2)
+        ga_t = sb("ga_t", [P, PACK], F32)
+        nc.sync.dma_start(ga_t[:], ga.rearrange("(p t) o -> p (t o)", t=PACK))
+        w2_raw = sb("w2_raw", [P, PACK, H], F32)
+        nc.sync.dma_start(w2_raw[:], w2.rearrange("(p j) c -> p j c", j=PACK))
+        gb_t = sb("gb_t", [P, PACK], F32)
+        nc.sync.dma_start(gb_t[:], gb.rearrange("(p t) o -> p (t o)", t=PACK))
+        nq_t = load_list("nq_t", nq)
+        cq_t = load_list("cq_t", cq)
+
+        key_win = [sb("key_win%d" % t, [P, WINDOW], F32) for t in range(PACK)]
+        query_win = [sb("query_win%d" % t, [P, WINDOW], F32) for t in range(2)]
+        for w in key_win + query_win:
+            nc.gpsimd.memset(w[:, S:], 0.0)
+
+        def gather(name, table, offsets, dtype):
+            g = sb(name, [P, S], dtype)
+            nc.vector.tensor_copy(g[:], table[:].indirect(offsets[:]))
+            return g
+
+        def cast_half(g, raw, h, copy):
+            copy(g.rearrange("p t (m j) -> p m j t", j=PACK), raw[:].rearrange("p j (m t) -> p m j t", t=PACK)[:, :, :, 2 * h : 2 * h + 2])
+            return g.rearrange("p t n -> p (t n)")
+
+        def quantise(name, grouped):
+            n = grouped.shape[1] // PACK
+            codes = sb(name + "_codes", [P, n], U32)
+            scales = sb(name + "_scales", [P, n], U8)
+            nc.vector.quantize_mx(out=codes[:].bitcast(FP8X4), scales=scales[:], in_=grouped)
+            return codes, scales
+
+        def product(tag, stationary, cols, moving):
+            acc = psum.tile([P, S], F32, name=tag, tag=tag)
+            nc.tensor.matmul_mx(out=acc[:], lhsT=stationary[0][:, cols].bitcast(FP8X4), lhsT_scale=stationary[1][:, cols],
+                                rhs=moving[0][:].bitcast(FP8X4), rhs_scale=moving[1][:], start=True, stop=True)
+            return acc
+
+        key_scales = gather("key_scales", scale_table, offs_t, U8)
+        query_scales = gather("query_scales", scale_table, two_t, U8)
+        w1_g = [sb("w1_g%d" % h, [P, 2, H], BF16) for h in range(2)]
+        w1_halves = [cast_half(w1_g[0][:], w1_raw, 0, nc.vector.tensor_copy), cast_half(w1_g[1][:], w1_raw, 1, nc.scalar.copy)]
+        w1_q = [quantise("w1_%d" % h, w1_halves[h]) for h in range(2)]
+        key_words = gather("key_words", word_table, offs_t, U32)
+        query_words = gather("query_words", word_table, two_t, U32)
+
+        half_cols = [slice(P * (t % 2), P * (t % 2 + 1)) for t in range(PACK)]
+        a_ps = [product("bank%d" % t, w1_q[t // 2], half_cols[t], (key_words, key_scales)) for t in range(PACK)]
+        fetched = sb("fetched", [P, PACK, 2, S], BF16)
+        k1 = fetched[:, :, 0, :]
+        k2 = fetched[:, :, 1, :]
+        w2_g = [fetched[:, 1], fetched[:, 2]]
+        w2_q = []
+        for t in range(PACK):
+            nc.scalar.activation(key_win[t][:, :S], a_ps[t][:], ACT.Copy, scale=ga_t[:, t : t + 1])
+            if t in (1, 2):
+                w2_q.append(quantise("w2_%d" % (t - 1), cast_half(w2_g[t - 1], w2_raw, t - 1, nc.scalar.copy)))
+            nc.vector.tensor_copy(k1[:, t, :], key_win[t][:].indirect(n1_t[:]))
+            nc.vector.tensor_copy(k2[:, t, :], key_win[t][:].indirect(n2_t[:]))
+
+        b_ps = [product("bank%d" % (PACK + t), w2_q[t // 2], half_cols[t], (query_words, query_scales)) for t in range(PACK)]
+        gate = sb("gate", [P, PACK, V], F32)
+        b_scaled = sb("b_scaled", [P, PACK, V], F32)
+        for t in range(PACK):
+            win = query_win[t % 2]
+            nc.scalar.copy(win[:, :V], b_ps[t][:])
+            nc.scalar.activation(b_scaled[:, t, :], b_ps[t][:], ACT.Copy, scale=gb_t[:, t : t + 1])
+            nc.scalar.activation(gate[:, t, :], win[:].indirect(nq_t[:]), ACT.Sigmoid)
+
+        high = sb("high", [P, PACK, S], BF16)
+        low = sb("low", [P, PACK, S], BF16)
+        mid = sb("mid", [P, PACK, S], BF16)
+        nc.vector.tensor_tensor(high[:], k1, k2, ALU.max)
+        nc.vector.tensor_tensor(low[:], k1, k2, ALU.min)
+        for t in range(PACK):
+            nc.vector.tensor_tensor(mid[:, t, :], high[:, t, :], key_win[t][:, :S], ALU.min)
+
+        def natural(x):
+            return x[:].rearrange("p t (q u c) -> p (t q) u c", u=PACK, c=8)
+
+        z_planes = sb("z_planes", [P, PACK, PACK, P], BF16)
+        dealt = z_planes[:].rearrange("p u t (q c) -> p (t q) u c", c=8)
+        z_all = sb("z_all", [P, PACK, P, PACK], BF16, tag="query_win1")
+        z_g = []
+        for u in range(PACK):
+            if u % 2 == 0:
+                nc.vector.tensor_tensor(dealt[:, :, u : u + 2], natural(low)[:, :, u : u + 2], natural(mid)[:, :, u : u + 2], ALU.max)
+            g = z_all[:, u]
+            nc.scalar.copy(g.rearrange("p (c i) t -> p c t i", i=4), z_planes[:, u].rearrange("p t (c i) -> p c t i", i=4))
+            z_g.append(g)
+        z2_g = sb("z2_g", [P, V, PACK], BF16)
+        nc.vector.tensor_tensor(z2_g[:].rearrange("p (c i) t -> p c t i", i=2), b_scaled[:].rearrange("p t (c i) -> p c t i", i=2),
+                                gate[:].rearrange("p t (c i) -> p c t i", i=2), ALU.mult)
+        z2_q = quantise("z2", z2_g[:].rearrange("p c t -> p (c t)"))
+        out_rows = out.rearrange("(q u c) v -> u q c v", u=PACK, c=8)
+        for u in range(PACK):
+            z_q = quantise("zk%d" % u, z_g[u].rearrange("p c t -> p (c t)"))
+            s_ps = product("bank%d" % u, z_q, slice(0, P), z2_q)
+            s_t = sb("s%d" % u, [P, V], F32)
+            nc.scalar.activation(key_win[u][:, :V], s_ps[:], ACT.Copy, scale=-0.03125)
+            nc.scalar.activation(s_t[:], s_ps[:], ACT.Copy, scale=0.0625)
+            pieces = 2 if u == PACK - 1 else 1
+            for h in range(pieces):
+                n = V // pieces
+                o_t = sb("o%d_%d" % (u, h), [P, n], F32)
+                nc.vector.tensor_tensor(o_t[:], key_win[u][:].indirect(cq_t[:, h * n // 16 : (h + 1) * n // 16]), s_t[:, h * n : (h + 1) * n], ALU.add)
+                nc.sync.dma_start(out_rows[u][:, :, h * n : (h + 1) * n], o_t[:])

@@ -35,9 +35,9 @@ def tile_picked_keymed_none_p_kernel(tc, x_words, x_scales, w1, w2, ga, gb, offs
             return t
 
         scale_table = sb("scale_table", [P, T], U8)
-        nc.vector.memset(scale_table[:].bitcast(I32), 0)
+        nc.gpsimd.memset(scale_table[:].bitcast(I32), 0)
         warm = sb("warm", [P, 2], F32)
-        nc.gpsimd.memset(warm[:, 0:1], 0.0)
+        nc.vector.memset(warm[:, 0:1], 0.0)
         nc.scalar.activation(warm[:, 1:2], warm[:, 0:1], ACT.Sigmoid)
 
         offs_t = load_list("offs_t", offs)
@@ -60,7 +60,7 @@ def tile_picked_keymed_none_p_kernel(tc, x_words, x_scales, w1, w2, ga, gb, offs
         cq_t = load_list("cq_t", cq)
 
         key_win = [sb("key_win%d" % t, [P, WINDOW], F32) for t in range(PACK)]
-        query_win = [sb("query_win%d" % t, [P, WINDOW], F32) for t in range(2)]
+        query_win = [sb("query_win%d" % t, [P, WINDOW], F32) for t in range(PACK)]
         for w in key_win + query_win:
             nc.gpsimd.memset(w[:, S:], 0.0)
 
@@ -110,37 +110,38 @@ def tile_picked_keymed_none_p_kernel(tc, x_words, x_scales, w1, w2, ga, gb, offs
 
         b_ps = [product("bank%d" % (PACK + t), w2_q[t // 2], half_cols[t], (query_words, query_scales)) for t in range(PACK)]
         gate = sb("gate", [P, PACK, V], F32)
-        b_scaled = sb("b_scaled", [P, PACK, V], F32)
+        z2_planes = sb("z2_planes", [P, PACK, V], BF16)
         for t in range(PACK):
-            win = query_win[t % 2]
+            win = query_win[t]
             nc.scalar.copy(win[:, :V], b_ps[t][:])
-            nc.scalar.activation(b_scaled[:, t, :], b_ps[t][:], ACT.Copy, scale=gb_t[:, t : t + 1])
             nc.scalar.activation(gate[:, t, :], win[:].indirect(nq_t[:]), ACT.Sigmoid)
+            nc.vector.scalar_tensor_tensor(z2_planes[:, t, :], b_ps[t][:], gb_t[:, t : t + 1], gate[:, t, :], ALU.mult, ALU.mult)
+        a_bf = sb("a_bf", [P, PACK, S], BF16)
+        for t in range(PACK):
+            nc.scalar.activation(a_bf[:, t, :], a_ps[t][:], ACT.Copy, scale=ga_t[:, t : t + 1])
+        z2_g = sb("z2_g", [P, V, PACK], BF16)
+        nc.scalar.copy(z2_g[:].rearrange("p (c i) t -> p c t i", i=4), z2_planes[:].rearrange("p t (c i) -> p c t i", i=4))
 
         high = sb("high", [P, PACK, S], BF16)
         low = sb("low", [P, PACK, S], BF16)
         mid = sb("mid", [P, PACK, S], BF16)
         nc.vector.tensor_tensor(high[:], k1, k2, ALU.max)
         nc.vector.tensor_tensor(low[:], k1, k2, ALU.min)
-        for t in range(PACK):
-            nc.vector.tensor_tensor(mid[:, t, :], high[:, t, :], key_win[t][:, :S], ALU.min)
+        nc.vector.tensor_tensor(mid[:], high[:], a_bf[:], ALU.min)
 
         def natural(x):
             return x[:].rearrange("p t (q u c) -> p (t q) u c", u=PACK, c=8)
 
         z_planes = sb("z_planes", [P, PACK, PACK, P], BF16)
         dealt = z_planes[:].rearrange("p u t (q c) -> p (t q) u c", c=8)
-        z_all = sb("z_all", [P, PACK, P, PACK], BF16, tag="query_win1")
+        z_all = sb("z_all", [P, PACK, P, PACK], BF16)
         z_g = []
         for u in range(PACK):
             if u % 2 == 0:
                 nc.vector.tensor_tensor(dealt[:, :, u : u + 2], natural(low)[:, :, u : u + 2], natural(mid)[:, :, u : u + 2], ALU.max)
             g = z_all[:, u]
-            nc.scalar.copy(g.rearrange("p (c i) t -> p c t i", i=4), z_planes[:, u].rearrange("p t (c i) -> p c t i", i=4))
+            nc.vector.tensor_copy(g.rearrange("p (c i) t -> p c t i", i=4), z_planes[:, u].rearrange("p t (c i) -> p c t i", i=4))
             z_g.append(g)
-        z2_g = sb("z2_g", [P, V, PACK], BF16)
-        nc.vector.tensor_tensor(z2_g[:].rearrange("p (c i) t -> p c t i", i=2), b_scaled[:].rearrange("p t (c i) -> p c t i", i=2),
-                                gate[:].rearrange("p t (c i) -> p c t i", i=2), ALU.mult)
         z2_q = quantise("z2", z2_g[:].rearrange("p c t -> p (c t)"))
         out_rows = out.rearrange("(q u c) v -> u q c v", u=PACK, c=8)
         for u in range(PACK):

@@ -41,21 +41,24 @@ def tile_picked_keymed_none_p_kernel(tc, x_words, x_scales, w1, w2, ga, gb, offs
         nc.scalar.activation(warm[:, 1:2], warm[:, 0:1], ACT.Sigmoid)
 
         offs_t = load_list("offs_t", offs)
-        two_t = load_list("two_t", two)
         for q in range(4):
             nc.sync.dma_start(scale_table[32 * q : 32 * q + 4, :].bitcast(I32), x_scales[0, 4 * q : 4 * q + 4, :].bitcast(I32))
+        two_t = load_list("two_t", two)
         w1_raw = sb("w1_raw", [P, PACK, H], F32)
         nc.sync.dma_start(w1_raw[:], w1.rearrange("(p j) c -> p j c", j=PACK))
         word_table = sb("word_table", [P, T], U32)
         nc.sync.dma_start(word_table[:].bitcast(I32), x_words[0].rearrange("p c r -> p (c r)").bitcast(I32))
+        def load_gain(name, src):
+            g = sb(name, [P, PACK], F32)
+            nc.sync.dma_start(g[:], src.rearrange("(p t) o -> p (t o)", t=PACK))
+            return g
+
         n1_t = load_list("n1_t", n1)
         n2_t = load_list("n2_t", n2)
-        ga_t = sb("ga_t", [P, PACK], F32)
-        nc.sync.dma_start(ga_t[:], ga.rearrange("(p t) o -> p (t o)", t=PACK))
+        ga_t = load_gain("ga_t", ga)
         w2_raw = sb("w2_raw", [P, PACK, H], F32)
         nc.sync.dma_start(w2_raw[:], w2.rearrange("(p j) c -> p j c", j=PACK))
-        gb_t = sb("gb_t", [P, PACK], F32)
-        nc.sync.dma_start(gb_t[:], gb.rearrange("(p t) o -> p (t o)", t=PACK))
+        gb_t = load_gain("gb_t", gb)
         nq_t = load_list("nq_t", nq)
         cq_t = load_list("cq_t", cq)
 
@@ -71,7 +74,7 @@ def tile_picked_keymed_none_p_kernel(tc, x_words, x_scales, w1, w2, ga, gb, offs
 
         def cast_half(g, raw, h, copy):
             copy(g.rearrange("p t (m j) -> p m j t", j=PACK), raw[:].rearrange("p j (m t) -> p m j t", t=PACK)[:, :, :, 2 * h : 2 * h + 2])
-            return g.rearrange("p t n -> p (t n)")
+            return g
 
         def quantise(name, grouped):
             n = grouped.shape[1] // PACK
@@ -80,45 +83,54 @@ def tile_picked_keymed_none_p_kernel(tc, x_words, x_scales, w1, w2, ga, gb, offs
             nc.vector.quantize_mx(out=codes[:].bitcast(FP8X4), scales=scales[:], in_=grouped)
             return codes, scales
 
-        def product(tag, stationary, cols, moving):
-            acc = psum.tile([P, S], F32, name=tag, tag=tag)
+        def product(tag, stationary, cols, moving, part=slice(0, S)):
+            acc = psum.tile([P, part.stop - part.start], F32, name=tag, tag=tag)
             nc.tensor.matmul_mx(out=acc[:], lhsT=stationary[0][:, cols].bitcast(FP8X4), lhsT_scale=stationary[1][:, cols],
-                                rhs=moving[0][:].bitcast(FP8X4), rhs_scale=moving[1][:], start=True, stop=True)
+                                rhs=moving[0][:, part].bitcast(FP8X4), rhs_scale=moving[1][:, part], start=True, stop=True)
             return acc
 
         key_scales = gather("key_scales", scale_table, offs_t, U8)
         query_scales = gather("query_scales", scale_table, two_t, U8)
         w1_g = [sb("w1_g%d" % h, [P, 2, H], BF16) for h in range(2)]
         w1_halves = [cast_half(w1_g[0][:], w1_raw, 0, nc.vector.tensor_copy), cast_half(w1_g[1][:], w1_raw, 1, nc.scalar.copy)]
-        w1_q = [quantise("w1_%d" % h, w1_halves[h]) for h in range(2)]
-        key_words = gather("key_words", word_table, offs_t, U32)
+        w1_q = [quantise("w1_%d" % h, w1_halves[h].rearrange("p t n -> p (t n)")) for h in range(2)]
+        key_words = sb("key_words", [P, S], U32)
+        for h in range(2):
+            nc.vector.tensor_copy(key_words[:, h * 256 : (h + 1) * 256], word_table[:].indirect(offs_t[:, h * 16 : (h + 1) * 16]))
         query_words = gather("query_words", word_table, two_t, U32)
 
         half_cols = [slice(P * (t % 2), P * (t % 2 + 1)) for t in range(PACK)]
-        a_ps = [product("bank%d" % t, w1_q[t // 2], half_cols[t], (key_words, key_scales)) for t in range(PACK)]
+        parts = [[slice(0, 256), slice(256, 512)]] + [[slice(0, S)]] * 3
+        a_ps = [[product("bank%d" % (t + 7 * h), w1_q[t // 2], half_cols[t], (key_words, key_scales), part) for h, part in enumerate(parts[t])] for t in range(PACK)]
+        a_bf = sb("a_bf", [P, PACK, S], BF16)
         fetched = sb("fetched", [P, PACK, 2, S], BF16)
         k1 = fetched[:, :, 0, :]
         k2 = fetched[:, :, 1, :]
         w2_g = [fetched[:, 1], fetched[:, 2]]
         w2_q = []
         for t in range(PACK):
-            nc.scalar.activation(key_win[t][:, :S], a_ps[t][:], ACT.Copy, scale=ga_t[:, t : t + 1])
+            for h, part in enumerate(parts[t]):
+                nc.scalar.activation(key_win[t][:, part], a_ps[t][h][:], ACT.Copy, scale=ga_t[:, t : t + 1])
+            nc.gpsimd.tensor_scalar(a_bf[:, t, :], key_win[t][:, :S], 1.0, 0.0, ALU.mult, ALU.add)
             if t in (1, 2):
-                w2_q.append(quantise("w2_%d" % (t - 1), cast_half(w2_g[t - 1], w2_raw, t - 1, nc.scalar.copy)))
+                g = cast_half(w2_g[t - 1], w2_raw, t - 1, nc.scalar.copy)
+                w2_q.extend(quantise("w2_%d" % (2 * (t - 1) + i), g[:, i, :]) for i in range(2))
             nc.vector.tensor_copy(k1[:, t, :], key_win[t][:].indirect(n1_t[:]))
             nc.vector.tensor_copy(k2[:, t, :], key_win[t][:].indirect(n2_t[:]))
 
-        b_ps = [product("bank%d" % (PACK + t), w2_q[t // 2], half_cols[t], (query_words, query_scales)) for t in range(PACK)]
+        b_ps = [product("bank%d" % (PACK + t), w2_q[t], slice(0, P), (query_words, query_scales)) for t in range(PACK)]
         gate = sb("gate", [P, PACK, V], F32)
         z2_planes = sb("z2_planes", [P, PACK, V], BF16)
         for t in range(PACK):
             win = query_win[t]
             nc.scalar.copy(win[:, :V], b_ps[t][:])
             nc.scalar.activation(gate[:, t, :], win[:].indirect(nq_t[:]), ACT.Sigmoid)
-            nc.vector.scalar_tensor_tensor(z2_planes[:, t, :], b_ps[t][:], gb_t[:, t : t + 1], gate[:, t, :], ALU.mult, ALU.mult)
-        a_bf = sb("a_bf", [P, PACK, S], BF16)
-        for t in range(PACK):
-            nc.scalar.activation(a_bf[:, t, :], a_ps[t][:], ACT.Copy, scale=ga_t[:, t : t + 1])
+            if t < 2:
+                scaled = sb("scaled%d" % t, [P, V], F32)
+                nc.gpsimd.tensor_scalar(scaled[:], win[:, :V], gb_t[:, t : t + 1], 0.0, ALU.mult, ALU.add)
+                nc.gpsimd.tensor_tensor(z2_planes[:, t, :], scaled[:], gate[:, t, :], ALU.mult)
+            else:
+                nc.vector.scalar_tensor_tensor(z2_planes[:, t, :], b_ps[t][:], gb_t[:, t : t + 1], gate[:, t, :], ALU.mult, ALU.mult)
         z2_g = sb("z2_g", [P, V, PACK], BF16)
         nc.scalar.copy(z2_g[:].rearrange("p (c i) t -> p c t i", i=4), z2_planes[:].rearrange("p t (c i) -> p c t i", i=4))
 
@@ -127,11 +139,12 @@ def tile_picked_keymed_none_p_kernel(tc, x_words, x_scales, w1, w2, ga, gb, offs
         mid = sb("mid", [P, PACK, S], BF16)
         nc.vector.tensor_tensor(high[:], k1, k2, ALU.max)
         nc.vector.tensor_tensor(low[:], k1, k2, ALU.min)
-        nc.vector.tensor_tensor(mid[:], high[:], a_bf[:], ALU.min)
 
         def natural(x):
             return x[:].rearrange("p t (q u c) -> p (t q) u c", u=PACK, c=8)
 
+        for u in (0, 2):
+            nc.vector.tensor_tensor(natural(mid)[:, :, u : u + 2], natural(high)[:, :, u : u + 2], natural(a_bf)[:, :, u : u + 2], ALU.min)
         z_planes = sb("z_planes", [P, PACK, PACK, P], BF16)
         dealt = z_planes[:].rearrange("p u t (q c) -> p (t q) u c", c=8)
         z_all = sb("z_all", [P, PACK, P, PACK], BF16)

@@ -100,72 +100,111 @@ def tile_picked_keymed_none_p_kernel(tc, x_words, x_scales, w1, w2, ga, gb, offs
         query_words = gather("query_words", word_table, two_t, U32)
 
         half_cols = [slice(P * (t % 2), P * (t % 2 + 1)) for t in range(PACK)]
-        parts = [[slice(0, 256), slice(256, 512)]] + [[slice(0, S)]] * 3
-        a_ps = [[product("bank%d" % (t + 7 * h), w1_q[t // 2], half_cols[t], (key_words, key_scales), part) for h, part in enumerate(parts[t])] for t in range(PACK)]
         a_bf = sb("a_bf", [P, PACK, S], BF16)
         fetched = sb("fetched", [P, PACK, 2, S], BF16)
         k1 = fetched[:, :, 0, :]
         k2 = fetched[:, :, 1, :]
-        w2_g = [fetched[:, 1], fetched[:, 2]]
+        gate = sb("gate", [P, PACK, V], F32)
+        z2_planes = sb("z2_planes", [P, PACK, V], BF16)
         w2_q = []
-        for t in range(PACK):
-            for h, part in enumerate(parts[t]):
-                nc.scalar.activation(key_win[t][:, part], a_ps[t][h][:], ACT.Copy, scale=ga_t[:, t : t + 1])
+        b_ps = []
+
+        def project_keys(t, banks):
+            n = S // len(banks)
+            for h, bank in enumerate(banks):
+                part = slice(h * n, (h + 1) * n)
+                acc = product(bank, w1_q[t // 2], half_cols[t], (key_words, key_scales), part)
+                nc.scalar.activation(key_win[t][:, part], acc[:], ACT.Copy, scale=ga_t[:, t : t + 1])
             nc.gpsimd.tensor_scalar(a_bf[:, t, :], key_win[t][:, :S], 1.0, 0.0, ALU.mult, ALU.add)
-            if t in (1, 2):
-                g = cast_half(w2_g[t - 1], w2_raw, t - 1, nc.scalar.copy)
-                w2_q.extend(quantise("w2_%d" % (2 * (t - 1) + i), g[:, i, :]) for i in range(2))
+
+        def fetch_keys(t):
             nc.vector.tensor_copy(k1[:, t, :], key_win[t][:].indirect(n1_t[:]))
             nc.vector.tensor_copy(k2[:, t, :], key_win[t][:].indirect(n2_t[:]))
 
-        b_ps = [product("bank%d" % (PACK + t), w2_q[t], slice(0, P), (query_words, query_scales)) for t in range(PACK)]
-        gate = sb("gate", [P, PACK, V], F32)
-        z2_planes = sb("z2_planes", [P, PACK, V], BF16)
-        for t in range(PACK):
-            win = query_win[t]
-            nc.scalar.copy(win[:, :V], b_ps[t][:])
-            nc.scalar.activation(gate[:, t, :], win[:].indirect(nq_t[:]), ACT.Sigmoid)
+        def quantise_w2(h):
+            g = cast_half(fetched[:, h + 1], w2_raw, h, nc.scalar.copy)
+            w2_q.extend(quantise("w2_%d" % (2 * h + i), g[:, i, :]) for i in range(2))
+
+        def project_queries(t):
+            b_ps.append(product("bank%d" % (PACK + t), w2_q[t], slice(0, P), (query_words, query_scales)))
+            nc.scalar.copy(query_win[t][:, :V], b_ps[t][:])
+
+        def gate_queries(t, lo=0, hi=V):
+            nc.scalar.activation(gate[:, t, lo:hi], query_win[t][:].indirect(nq_t[:, lo // 16 : hi // 16]), ACT.Sigmoid)
             if t < 2:
                 scaled = sb("scaled%d" % t, [P, V], F32)
-                nc.gpsimd.tensor_scalar(scaled[:], win[:, :V], gb_t[:, t : t + 1], 0.0, ALU.mult, ALU.add)
+                nc.gpsimd.tensor_scalar(scaled[:], query_win[t][:, :V], gb_t[:, t : t + 1], 0.0, ALU.mult, ALU.add)
                 nc.gpsimd.tensor_tensor(z2_planes[:, t, :], scaled[:], gate[:, t, :], ALU.mult)
             else:
-                nc.vector.scalar_tensor_tensor(z2_planes[:, t, :], b_ps[t][:], gb_t[:, t : t + 1], gate[:, t, :], ALU.mult, ALU.mult)
+                nc.vector.scalar_tensor_tensor(z2_planes[:, t, lo:hi], b_ps[t][:, lo:hi], gb_t[:, t : t + 1], gate[:, t, lo:hi], ALU.mult, ALU.mult)
+
+        project_keys(0, ["bank0", "bank3"])
+        fetch_keys(0)
+        project_keys(1, ["bank1"])
+        quantise_w2(0)
+        fetch_keys(1)
+        project_keys(2, ["bank2"])
+        quantise_w2(1)
+        fetch_keys(2)
+        project_queries(0)
+        project_keys(3, ["bank4"])
+        fetch_keys(3)
+        project_queries(1)
+        gate_queries(0)
+        gate_queries(1)
+        project_queries(2)
+        project_queries(3)
+        gate_queries(2)
+        gate_queries(3, 0, V // 2)
+        gate_queries(3, V // 2, V)
         z2_g = sb("z2_g", [P, V, PACK], BF16)
-        nc.scalar.copy(z2_g[:].rearrange("p (c i) t -> p c t i", i=4), z2_planes[:].rearrange("p t (c i) -> p c t i", i=4))
+        for h in range(2):
+            cols = slice(h * V // 2, (h + 1) * V // 2)
+            nc.scalar.copy(z2_g[:, cols, :].rearrange("p (c i) t -> p c t i", i=4), z2_planes[:, :, cols].rearrange("p t (c i) -> p c t i", i=4))
+
+        def keys(x, h):
+            return x.rearrange("p t (q u c) -> p (t q) u c", u=PACK, c=8)[:, :, 2 * h : 2 * h + 2]
 
         high = sb("high", [P, PACK, S], BF16)
-        low = sb("low", [P, PACK, S], BF16)
-        mid = sb("mid", [P, PACK, S], BF16)
+        mid_first = sb("mid_first", [P, 2 * S], BF16)
+        after_gate = sb("after_gate", [P, 6 * S], BF16, tag="gate")
+        low = after_gate[:, : 4 * S].rearrange("p (t s) -> p t s", t=PACK)
+        mid = [m.rearrange("p (n u c) -> p n u c", u=2, c=8) for m in (mid_first[:], after_gate[:, 4 * S :])]
         nc.vector.tensor_tensor(high[:], k1, k2, ALU.max)
-        nc.vector.tensor_tensor(low[:], k1, k2, ALU.min)
+        nc.vector.tensor_tensor(mid[0], keys(high[:], 0), keys(a_bf[:], 0), ALU.min)
+        nc.vector.tensor_tensor(low, k1, k2, ALU.min)
+        nc.vector.tensor_tensor(mid[1], keys(high[:], 1), keys(a_bf[:], 1), ALU.min)
 
-        def natural(x):
-            return x[:].rearrange("p t (q u c) -> p (t q) u c", u=PACK, c=8)
+        def median(planes, h):
+            nc.vector.tensor_tensor(planes.rearrange("p (u n c) -> p n u c", u=2, c=8), keys(low, h), mid[h], ALU.max)
 
-        for u in (0, 2):
-            nc.vector.tensor_tensor(natural(mid)[:, :, u : u + 2], natural(high)[:, :, u : u + 2], natural(a_bf)[:, :, u : u + 2], ALU.min)
-        z_planes = sb("z_planes", [P, PACK, PACK, P], BF16)
-        dealt = z_planes[:].rearrange("p u t (q c) -> p (t q) u c", c=8)
-        z_all = sb("z_all", [P, PACK, P, PACK], BF16)
-        z_g = []
-        for u in range(PACK):
-            if u % 2 == 0:
-                nc.vector.tensor_tensor(dealt[:, :, u : u + 2], natural(low)[:, :, u : u + 2], natural(mid)[:, :, u : u + 2], ALU.max)
-            g = z_all[:, u]
-            nc.vector.tensor_copy(g.rearrange("p (c i) t -> p c t i", i=4), z_planes[:, u].rearrange("p t (c i) -> p c t i", i=4))
-            z_g.append(g)
-        z2_q = quantise("z2", z2_g[:].rearrange("p c t -> p (c t)"))
+        def interleave(dst, planes):
+            nc.vector.tensor_copy(dst.rearrange("p (c i t) -> p c t i", i=4, t=PACK), planes.rearrange("p (t c i) -> p c t i", i=4, t=PACK))
+
+        z_first = sb("z_first", [P, 3 * S], BF16)
+        median(z_first[:, : 2 * S], 0)
+        interleave(z_first[:, 2 * S :], z_first[:, :S])
+        z2_q = (sb("z2_codes", [P, V], U32), sb("z2_scales", [P, V], U8))
+        for h in range(2):
+            cols = slice(h * V // 2, (h + 1) * V // 2)
+            nc.vector.quantize_mx(out=z2_q[0][:, cols].bitcast(FP8X4), scales=z2_q[1][:, cols], in_=z2_g[:, cols, :].rearrange("p c t -> p (c t)"))
+        z_q = [quantise("zk0", z_first[:, 2 * S :])]
+        z_rest = sb("z_rest", [P, 5 * S], BF16, tag="z2_g")
+        median(z_rest[:, : 2 * S], 1)
+        planes = [z_first[:, S : 2 * S], z_rest[:, :S], z_rest[:, S : 2 * S]]
+        for u in range(1, PACK):
+            interleave(z_rest[:, (u + 1) * S : (u + 2) * S], planes[u - 1])
+        for u in range(1, PACK):
+            z_q.append(quantise("zk%d" % u, z_rest[:, (u + 1) * S : (u + 2) * S]))
         out_rows = out.rearrange("(q u c) v -> u q c v", u=PACK, c=8)
+        last_win = sb("last_win", [P, V], F32)
         for u in range(PACK):
-            z_q = quantise("zk%d" % u, z_g[u].rearrange("p c t -> p (c t)"))
-            s_ps = product("bank%d" % u, z_q, slice(0, P), z2_q)
+            s_ps = product("bank%d" % u, z_q[u], slice(0, P), z2_q)
             s_t = sb("s%d" % u, [P, V], F32)
-            nc.scalar.activation(key_win[u][:, :V], s_ps[:], ACT.Copy, scale=-0.03125)
+            win = key_win[u] if u < PACK - 1 else last_win
+            nc.scalar.activation(win[:, :V], s_ps[:], ACT.Copy, scale=-0.03125)
             nc.scalar.activation(s_t[:], s_ps[:], ACT.Copy, scale=0.0625)
-            pieces = 2 if u == PACK - 1 else 1
-            for h in range(pieces):
-                n = V // pieces
-                o_t = sb("o%d_%d" % (u, h), [P, n], F32)
-                nc.vector.tensor_tensor(o_t[:], key_win[u][:].indirect(cq_t[:, h * n // 16 : (h + 1) * n // 16]), s_t[:, h * n : (h + 1) * n], ALU.add)
-                nc.sync.dma_start(out_rows[u][:, :, h * n : (h + 1) * n], o_t[:])
+            for lo, hi in [(0, V)] if u < PACK - 1 else [(0, 256), (256, 384), (384, V)]:
+                o_t = sb("o%d_%d" % (u, lo), [P, hi - lo], F32)
+                nc.vector.tensor_tensor(o_t[:], win[:].indirect(cq_t[:, lo // 16 : hi // 16]), s_t[:, lo:hi], ALU.add)
+                nc.sync.dma_start(out_rows[u][:, :, lo:hi], o_t[:])

from contextlib import ExitStack

import concourse.mybir as mybir

K, T, S, V, H = 512, 2048, 512, 512, 512
FLOPS = 2 * K * H * S + 2 * K * H * V + 2 * H * S * V

F32 = mybir.dt.float32
BF16 = mybir.dt.bfloat16
I32 = mybir.dt.int32
U32 = mybir.dt.uint32
U16 = mybir.dt.uint16
U8 = mybir.dt.uint8
FP8X4 = mybir.dt.float8_e4m3fn_x4
ALU = mybir.AluOpType
ACT = mybir.ActivationFunctionType

P = 128
PACK = 4
WINDOW = 1024


def tile_picked_keymed_none_p_kernel(tc, x_words, x_scales, w1, w2, ga, gb, offs, two, n1, n2, nq, cq, out):
    nc = tc.nc
    with ExitStack() as ctx:
        keep = ctx.enter_context(tc.tile_pool(name="keep", bufs=1))
        psum = ctx.enter_context(tc.psum_pool(name="psum", bufs=1))

        def sb(name, shape, dtype, tag=None):
            return keep.tile(shape, dtype, name=name, tag=tag or name, align_bytes=64)

        def load_list(name, src):
            t = keep.tile([P, 32], U16, name=name)
            nc.sync.dma_start(t[:], src)
            return t

        scale_table = sb("scale_table", [P, T], U8)
        nc.gpsimd.memset(scale_table[:].bitcast(I32), 0)
        warm = sb("warm", [P, 2], F32)
        nc.vector.memset(warm[:, 0:1], 0.0)
        nc.scalar.activation(warm[:, 1:2], warm[:, 0:1], ACT.Sigmoid)

        offs_t = load_list("offs_t", offs)
        for q in range(4):
            nc.sync.dma_start(scale_table[32 * q : 32 * q + 4, :].bitcast(I32), x_scales[0, 4 * q : 4 * q + 4, :].bitcast(I32))
        two_t = load_list("two_t", two)
        w1_raw = sb("w1_raw", [P, PACK, H], F32)
        nc.sync.dma_start(w1_raw[:], w1.rearrange("(p j) c -> p j c", j=PACK))
        word_table = sb("word_table", [P, T], U32)
        nc.sync.dma_start(word_table[:].bitcast(I32), x_words[0].rearrange("p c r -> p (c r)").bitcast(I32))
        def load_gain(name, src):
            g = sb(name, [P, PACK], F32)
            nc.sync.dma_start(g[:], src.rearrange("(p t) o -> p (t o)", t=PACK))
            return g

        n1_t = load_list("n1_t", n1)
        n2_t = load_list("n2_t", n2)
        ga_t = load_gain("ga_t", ga)
        w2_raw = sb("w2_raw", [P, PACK, H], F32)
        nc.sync.dma_start(w2_raw[:], w2.rearrange("(p j) c -> p j c", j=PACK))
        gb_t = load_gain("gb_t", gb)
        nq_t = load_list("nq_t", nq)
        cq_t = load_list("cq_t", cq)

        key_win = [sb("key_win%d" % t, [P, WINDOW], F32) for t in range(PACK)]
        query_win = [sb("query_win%d" % t, [P, WINDOW], F32) for t in range(PACK)]
        for w in key_win + query_win:
            nc.gpsimd.memset(w[:, S:], 0.0)

        def gather(name, table, offsets, dtype):
            g = sb(name, [P, S], dtype)
            nc.vector.tensor_copy(g[:], table[:].indirect(offsets[:]))
            return g

        def cast_half(g, raw, h, copy):
            copy(g.rearrange("p t (m j) -> p m j t", j=PACK), raw[:].rearrange("p j (m t) -> p m j t", t=PACK)[:, :, :, 2 * h : 2 * h + 2])
            return g

        def quantise(name, grouped):
            n = grouped.shape[1] // PACK
            codes = sb(name + "_codes", [P, n], U32)
            scales = sb(name + "_scales", [P, n], U8)
            nc.vector.quantize_mx(out=codes[:].bitcast(FP8X4), scales=scales[:], in_=grouped)
            return codes, scales

        def product(tag, stationary, cols, moving, part=slice(0, S)):
            acc = psum.tile([P, part.stop - part.start], F32, name=tag, tag=tag)
            nc.tensor.matmul_mx(out=acc[:], lhsT=stationary[0][:, cols].bitcast(FP8X4), lhsT_scale=stationary[1][:, cols],
                                rhs=moving[0][:, part].bitcast(FP8X4), rhs_scale=moving[1][:, part], start=True, stop=True)
            return acc

        key_scales = gather("key_scales", scale_table, offs_t, U8)
        query_scales = gather("query_scales", scale_table, two_t, U8)
        w1_g = [sb("w1_g%d" % h, [P, 2, H], BF16) for h in range(2)]
        w1_halves = [cast_half(w1_g[0][:], w1_raw, 0, nc.vector.tensor_copy), cast_half(w1_g[1][:], w1_raw, 1, nc.scalar.copy)]
        w1_q = [quantise("w1_%d" % h, w1_halves[h].rearrange("p t n -> p (t n)")) for h in range(2)]
        key_words = sb("key_words", [P, S], U32)
        for h in range(2):
            nc.vector.tensor_copy(key_words[:, h * 256 : (h + 1) * 256], word_table[:].indirect(offs_t[:, h * 16 : (h + 1) * 16]))
        query_words = gather("query_words", word_table, two_t, U32)

        half_cols = [slice(P * (t % 2), P * (t % 2 + 1)) for t in range(PACK)]
        a_bf = sb("a_bf", [P, PACK, S], BF16)
        fetched = sb("fetched", [P, PACK, 2, S], BF16)
        k1 = fetched[:, :, 0, :]
        k2 = fetched[:, :, 1, :]
        gate = sb("gate", [P, PACK, V], F32)
        z2_planes = sb("z2_planes", [P, PACK, V], BF16)
        w2_q = []
        b_ps = []

        def project_keys(t, banks):
            n = S // len(banks)
            for h, bank in enumerate(banks):
                part = slice(h * n, (h + 1) * n)
                acc = product(bank, w1_q[t // 2], half_cols[t], (key_words, key_scales), part)
                nc.scalar.activation(key_win[t][:, part], acc[:], ACT.Copy, scale=ga_t[:, t : t + 1])
            nc.gpsimd.tensor_scalar(a_bf[:, t, :], key_win[t][:, :S], 1.0, 0.0, ALU.mult, ALU.add)

        def fetch_keys(t):
            nc.vector.tensor_copy(k1[:, t, :], key_win[t][:].indirect(n1_t[:]))
            nc.vector.tensor_copy(k2[:, t, :], key_win[t][:].indirect(n2_t[:]))

        def quantise_w2(h):
            g = cast_half(fetched[:, h + 1], w2_raw, h, nc.scalar.copy)
            w2_q.extend(quantise("w2_%d" % (2 * h + i), g[:, i, :]) for i in range(2))

        def project_queries(t):
            b_ps.append(product("bank%d" % (PACK + t), w2_q[t], slice(0, P), (query_words, query_scales)))
            nc.scalar.copy(query_win[t][:, :V], b_ps[t][:])

        def gate_queries(t, lo=0, hi=V):
            nc.scalar.activation(gate[:, t, lo:hi], query_win[t][:].indirect(nq_t[:, lo // 16 : hi // 16]), ACT.Sigmoid)
            if t < 2:
                scaled = sb("scaled%d" % t, [P, V], F32)
                nc.gpsimd.tensor_scalar(scaled[:], query_win[t][:, :V], gb_t[:, t : t + 1], 0.0, ALU.mult, ALU.add)
                nc.gpsimd.tensor_tensor(z2_planes[:, t, :], scaled[:], gate[:, t, :], ALU.mult)
            else:
                nc.vector.scalar_tensor_tensor(z2_planes[:, t, lo:hi], b_ps[t][:, lo:hi], gb_t[:, t : t + 1], gate[:, t, lo:hi], ALU.mult, ALU.mult)

        project_keys(0, ["bank0", "bank3"])
        fetch_keys(0)
        project_keys(1, ["bank1"])
        quantise_w2(0)
        fetch_keys(1)
        project_keys(2, ["bank2"])
        quantise_w2(1)
        fetch_keys(2)
        project_queries(0)
        project_keys(3, ["bank4"])
        fetch_keys(3)
        project_queries(1)
        gate_queries(0)
        gate_queries(1)
        project_queries(2)
        project_queries(3)
        gate_queries(2)
        gate_queries(3, 0, V // 2)
        gate_queries(3, V // 2, V)
        z2_g = sb("z2_g", [P, V, PACK], BF16)
        for h in range(2):
            cols = slice(h * V // 2, (h + 1) * V // 2)
            nc.scalar.copy(z2_g[:, cols, :].rearrange("p (c i) t -> p c t i", i=4), z2_planes[:, :, cols].rearrange("p t (c i) -> p c t i", i=4))

        def keys(x, h):
            return x.rearrange("p t (q u c) -> p (t q) u c", u=PACK, c=8)[:, :, 2 * h : 2 * h + 2]

        high = sb("high", [P, PACK, S], BF16)
        mid_first = sb("mid_first", [P, 2 * S], BF16)
        after_gate = sb("after_gate", [P, 6 * S], BF16, tag="gate")
        low = after_gate[:, : 4 * S].rearrange("p (t s) -> p t s", t=PACK)
        mid = [m.rearrange("p (n u c) -> p n u c", u=2, c=8) for m in (mid_first[:], after_gate[:, 4 * S :])]
        nc.vector.tensor_tensor(high[:], k1, k2, ALU.max)
        nc.vector.tensor_tensor(mid[0], keys(high[:], 0), keys(a_bf[:], 0), ALU.min)
        nc.vector.tensor_tensor(low, k1, k2, ALU.min)
        nc.vector.tensor_tensor(mid[1], keys(high[:], 1), keys(a_bf[:], 1), ALU.min)

        def median(planes, h):
            nc.vector.tensor_tensor(planes.rearrange("p (u n c) -> p n u c", u=2, c=8), keys(low, h), mid[h], ALU.max)

        def interleave(dst, planes):
            nc.vector.tensor_copy(dst.rearrange("p (c i t) -> p c t i", i=4, t=PACK), planes.rearrange("p (t c i) -> p c t i", i=4, t=PACK))

        z_first = sb("z_first", [P, 3 * S], BF16)
        median(z_first[:, : 2 * S], 0)
        interleave(z_first[:, 2 * S :], z_first[:, :S])
        z2_q = (sb("z2_codes", [P, V], U32), sb("z2_scales", [P, V], U8))
        for h in range(2):
            cols = slice(h * V // 2, (h + 1) * V // 2)
            nc.vector.quantize_mx(out=z2_q[0][:, cols].bitcast(FP8X4), scales=z2_q[1][:, cols], in_=z2_g[:, cols, :].rearrange("p c t -> p (c t)"))
        z_q = [quantise("zk0", z_first[:, 2 * S :])]
        z_rest = sb("z_rest", [P, 5 * S], BF16, tag="z2_g")
        median(z_rest[:, : 2 * S], 1)
        planes = [z_first[:, S : 2 * S], z_rest[:, :S], z_rest[:, S : 2 * S]]
        for u in range(1, PACK):
            interleave(z_rest[:, (u + 1) * S : (u + 2) * S], planes[u - 1])
        for u in range(1, PACK):
            z_q.append(quantise("zk%d" % u, z_rest[:, (u + 1) * S : (u + 2) * S]))
        out_rows = out.rearrange("(q u c) v -> u q c v", u=PACK, c=8)
        last_win = sb("last_win", [P, V], F32)
        for u in range(PACK):
            s_ps = product("bank%d" % u, z_q[u], slice(0, P), z2_q)
            s_t = sb("s%d" % u, [P, V], F32)
            win = key_win[u] if u < PACK - 1 else last_win
            nc.scalar.activation(win[:, :V], s_ps[:], ACT.Copy, scale=-0.03125)
            nc.scalar.activation(s_t[:], s_ps[:], ACT.Copy, scale=0.0625)
            for lo, hi in [(0, V)] if u < PACK - 1 else [(0, 256), (256, 384), (384, V)]:
                o_t = sb("o%d_%d" % (u, lo), [P, hi - lo], F32)
                nc.vector.tensor_tensor(o_t[:], win[:].indirect(cq_t[:, lo // 16 : hi // 16]), s_t[:, lo:hi], ALU.add)
                nc.sync.dma_start(out_rows[u][:, :, lo:hi], o_t[:])
